import numpy as np
CORES = [5,13,21,29,133,141,149,157,261,269,277,285,389,397,405,413]
N = 16
ROOT = 10
def setup_inputs(rng):
    return {"x": rng.standard_normal((N, 128, 1024), dtype=np.float32)}
def reference(x):
    return {"y": np.broadcast_to(x[ROOT], x.shape)}

@@ -1,0 +1,107 @@
+import concourse.bass as bass
+import comms_topo
+
+ROOT = 277
+P = 1
+W = 1024 // P
+R = 128 // P
+VARIANT = "naive"
+
+SCRATCH = {"d": ("dram", [P, 128, W], "float32")}
+SEMAPHORES = ["a0", "a1", "a2", "a3", "a4", "a5", "a6", "a7", "a8", "a9", "a10", "a11", "a12", "a13", "a14", "a15",
+              "l0", "l1", "l2", "l3", "l4", "l5", "l6", "l7", "sent", "st"]
+
+
+def wc(h, c, k):
+    return h * 128 + c * 8 + k
+
+
+def plan():
+    kids, sched = {}, {}
+    if VARIANT == "naive":
+        for (h, o) in ((2, 3), (1, 0)):
+            top = wc(h, 2, 5)
+            kids[(top, 0)] = ([wc(1, 2, 5)] if h == 2 else []) + [wc(h, 2, 6), wc(h, 0, 5), wc(o, 0, 5), wc(o, 2, 5)]
+            kids[(wc(h, 2, 6), 0)] = [wc(h, 3, 5), wc(h, 1, 5), wc(o, 1, 5), wc(o, 3, 5)]
+            sched[wc(h, 2, 6)] = [[0]]
+            for hh in (h, o):
+                for c in range(4):
+                    sched[wc(hh, c, 5)] = [[0]]
+    return kids, sched
+
+
+def transfers(core, grp, kids):
+    send = [p for p in grp if kids.get((core, p))]
+    if not send:
+        return []
+    avail = 0xFFFF
+    for p in send:
+        for d in kids[(core, p)]:
+            avail &= comms_topo.mask(core, d)
+    n = 16 if avail == 0xFFFF else 8
+    e = 1
+    while e * 2 * len(send) <= n:
+        e *= 2
+    return [(p, kids[(core, p)], ((1 << e) - 1) << (i * e), e) for i, p in enumerate(send)]
+
+
+def runs(grp):
+    out = []
+    for p in sorted(grp):
+        if out and out[-1][1] == p:
+            out[-1][1] = p + 1
+        else:
+            out.append([p, p + 1])
+    return out
+
+
+def rank_program(g, core, T, topo):
+    kids, sched = plan()
+    my = sched.get(core)
+    if not my:
+        return
+    inc = {}
+    for src, groups in sched.items():
+        for grp in groups:
+            for (p, dsts, m, e) in transfers(src, grp, kids):
+                if core in dsts:
+                    inc[p] = e
+    A = [T.sem.a0, T.sem.a1, T.sem.a2, T.sem.a3, T.sem.a4, T.sem.a5, T.sem.a6, T.sem.a7,
+         T.sem.a8, T.sem.a9, T.sem.a10, T.sem.a11, T.sem.a12, T.sem.a13, T.sem.a14, T.sem.a15]
+    L = [T.sem.l0, T.sem.l1, T.sem.l2, T.sem.l3, T.sem.l4, T.sem.l5, T.sem.l6, T.sem.l7]
+    is_root = core == ROOT
+    is_rank = T.rank_of(core) is not None
+    sent = stores = 0
+    if is_root:
+        for gi, grp in enumerate(my):
+            lo, hi = grp[0], grp[-1] + 1
+            g.dma_start(T.d[lo:hi], T.x[lo * R:hi * R, :]).then_inc(L[gi], 16)
+    for gi, grp in enumerate(my):
+        if is_root:
+            g.wait_ge(L[gi], 16)
+        else:
+            for p in grp:
+                g.wait_ge(A[p], inc[p])
+        trs = transfers(core, grp, kids)
+        if trs:
+            calls = []
+            for (p, dsts, m, e) in trs:
+                ids = []
+                for d in dsts:
+                    rid, pid = topo.addr(d, core)
+                    ids.append(bass.DstId(rid=rid, pnc=pid))
+                calls.append(bass.RemoteDMATransfer(dst_ids=ids, dma_engine_mask=m, remote_sem=A[p],
+                                                    srcs=[T.d[p]], dsts=[T.d[p] for d in dsts]))
+                sent += e
+            g.remote_dma_fused(calls, local_sem=T.sem.sent)
+        if is_rank and not is_root:
+            for lo, hi in runs(grp):
+                g.dma_start(T.y[lo * R:hi * R, :], T.d[lo:hi]).then_inc(T.sem.st, 16)
+                stores += 1
+    if is_root:
+        g.dma_start(T.y[:, :], T.x[:, :]).then_inc(T.sem.st, 16)
+        stores += 1
+    if sent:
+        g.wait_ge(T.sem.sent, sent)
+    if stores:
+        g.wait_ge(T.sem.st, 16 * stores)

@@ -2,10 +2,11 @@ import concourse.bass as bass
 import comms_topo
 
 ROOT = 277
-P = 1
+P = 8
 W = 1024 // P
 R = 128 // P
-VARIANT = "naive"
+VARIANT = "ht"
+K4 = (2, 3, 6, 7)
 
 SCRATCH = {"d": ("dram", [P, 128, W], "float32")}
 SEMAPHORES = ["a0", "a1", "a2", "a3", "a4", "a5", "a6", "a7", "a8", "a9", "a10", "a11", "a12", "a13", "a14", "a15",
@@ -18,15 +19,59 @@ def wc(h, c, k):
 
 def plan():
     kids, sched = {}, {}
-    if VARIANT == "naive":
-        for (h, o) in ((2, 3), (1, 0)):
-            top = wc(h, 2, 5)
-            kids[(top, 0)] = ([wc(1, 2, 5)] if h == 2 else []) + [wc(h, 2, 6), wc(h, 0, 5), wc(o, 0, 5), wc(o, 2, 5)]
-            kids[(wc(h, 2, 6), 0)] = [wc(h, 3, 5), wc(h, 1, 5), wc(o, 1, 5), wc(o, 3, 5)]
-            sched[wc(h, 2, 6)] = [[0]]
-            for hh in (h, o):
-                for c in range(4):
-                    sched[wc(hh, c, 5)] = [[0]]
+    waves = [list(range(4 * w, 4 * w + 4)) for w in range(P // 4)]
+    mine = {k: [[p] for p in range(P) if K4[p % 4] == k] for k in K4}
+    for h in range(4):
+        for c in range(4):
+            sched[wc(h, c, 5)] = waves
+    if VARIANT == "flat":
+        for p in range(P):
+            k = K4[p % 4]
+            kids[(ROOT, p)] = [wc(2, 2, k)]
+            kids[(wc(2, 2, k), p)] = [wc(1, 2, k)] + [wc(h, c, 5) for (h, c) in
+                                                     ((3, 2), (3, 3), (3, 0), (3, 1), (2, 0), (2, 1), (2, 3))]
+            kids[(wc(1, 2, k), p)] = [wc(h, c, 5) for (h, c) in
+                                      ((0, 2), (0, 3), (0, 0), (0, 1), (1, 0), (1, 1), (1, 3), (1, 2))]
+        for k in K4:
+            sched[wc(2, 2, k)] = mine[k]
+            sched[wc(1, 2, k)] = mine[k]
+    if VARIANT == "ht":
+        for p in range(P):
+            k = K4[p % 4]
+            kids[(ROOT, p)] = [wc(2, 2, k)]
+            kids[(wc(2, 2, k), p)] = [wc(3, 2, k), wc(3, 0, k), wc(2, 0, k), wc(1, 2, k), wc(2, 3, 5)]
+            for (h, c) in ((3, 2), (3, 0), (2, 0)):
+                kids[(wc(h, c, k), p)] = [wc(3 - h, c, k), wc(h, c + 1, 5), wc(h, c, 5)]
+            for (h, c) in ((1, 2), (0, 2), (0, 0), (1, 0)):
+                kids[(wc(h, c, k), p)] = [wc(h, c + 1, 5), wc(h, c, 5)]
+        for k in K4:
+            for h in range(4):
+                for c in (0, 2):
+                    sched[wc(h, c, k)] = mine[k]
+    if VARIANT == "htr":
+        for p in range(P):
+            ki = p % 4
+            k = K4[ki]
+            kids[(ROOT, p)] = [wc(2, 2, k)]
+            for (h, o) in ((2, 3), (1, 0)):
+                relays = [(o, 2), (o, 0), (h, 0), (h, 4)]
+                r = relays[(p // 4 + ki) % 4]
+                kids[(wc(h, 2, k), p)] = ([wc(1, 2, k)] if h == 2 else []) + [wc(r[0], r[1], k), wc(h, 3, 5)] + (
+                    [wc(1, 2, 5)] if h == 1 else [])
+                for e in relays:
+                    kk = []
+                    if e == r:
+                        kk += [wc(q[0], q[1], k) for q in relays[:3] if q != e]
+                    if e != relays[3]:
+                        kk += [wc(e[0], e[1] + 1, 5), wc(e[0], e[1], 5)]
+                    if kk:
+                        kids[(wc(e[0], e[1], k), p)] = kk
+        for k in K4:
+            for h in range(4):
+                for c in (0, 2):
+                    sched[wc(h, c, k)] = mine[k]
+            for h in (2, 1):
+                sched[wc(h, 4, k)] = [[p] for [p] in mine[k] if kids.get((wc(h, 4, k), p))]
     return kids, sched
 
 

@@ -2,7 +2,7 @@ import concourse.bass as bass
 import comms_topo
 
 ROOT = 277
-P = 8
+P = 16
 W = 1024 // P
 R = 128 // P
 VARIANT = "ht"
@@ -24,17 +24,6 @@ def plan():
     for h in range(4):
         for c in range(4):
             sched[wc(h, c, 5)] = waves
-    if VARIANT == "flat":
-        for p in range(P):
-            k = K4[p % 4]
-            kids[(ROOT, p)] = [wc(2, 2, k)]
-            kids[(wc(2, 2, k), p)] = [wc(1, 2, k)] + [wc(h, c, 5) for (h, c) in
-                                                     ((3, 2), (3, 3), (3, 0), (3, 1), (2, 0), (2, 1), (2, 3))]
-            kids[(wc(1, 2, k), p)] = [wc(h, c, 5) for (h, c) in
-                                      ((0, 2), (0, 3), (0, 0), (0, 1), (1, 0), (1, 1), (1, 3), (1, 2))]
-        for k in K4:
-            sched[wc(2, 2, k)] = mine[k]
-            sched[wc(1, 2, k)] = mine[k]
     if VARIANT == "ht":
         for p in range(P):
             k = K4[p % 4]

@@ -2,15 +2,18 @@ import concourse.bass as bass
 import comms_topo
 
 ROOT = 277
-P = 16
+P = 32
+NW = 4
+PW = P // NW
 W = 1024 // P
 R = 128 // P
-VARIANT = "ht"
 K4 = (2, 3, 6, 7)
+HELP = (0, 2, 4, 6)
+NEAR = ((3, 0), (3, 2), (3, 4), (3, 6), (2, 0), (2, 4), (2, 6), (2, 8))
+FAR = ((1, 2), (1, 0), (1, 4), (1, 6), (1, 8), (1, 10), (1, 12), (1, 14))
 
 SCRATCH = {"d": ("dram", [P, 128, W], "float32")}
-SEMAPHORES = ["a0", "a1", "a2", "a3", "a4", "a5", "a6", "a7", "a8", "a9", "a10", "a11", "a12", "a13", "a14", "a15",
-              "l0", "l1", "l2", "l3", "l4", "l5", "l6", "l7", "sent", "st"]
+SEMAPHORES = ["a0", "a1", "a2", "a3", "l0", "l1", "l2", "l3", "sent", "st"]
 
 
 def wc(h, c, k):
@@ -19,48 +22,24 @@ def wc(h, c, k):
 
 def plan():
     kids, sched = {}, {}
-    waves = [list(range(4 * w, 4 * w + 4)) for w in range(P // 4)]
-    mine = {k: [[p] for p in range(P) if K4[p % 4] == k] for k in K4}
     for h in range(4):
         for c in range(4):
-            sched[wc(h, c, 5)] = waves
-    if VARIANT == "ht":
-        for p in range(P):
-            k = K4[p % 4]
-            kids[(ROOT, p)] = [wc(2, 2, k)]
-            kids[(wc(2, 2, k), p)] = [wc(3, 2, k), wc(3, 0, k), wc(2, 0, k), wc(1, 2, k), wc(2, 3, 5)]
-            for (h, c) in ((3, 2), (3, 0), (2, 0)):
-                kids[(wc(h, c, k), p)] = [wc(3 - h, c, k), wc(h, c + 1, 5), wc(h, c, 5)]
-            for (h, c) in ((1, 2), (0, 2), (0, 0), (1, 0)):
-                kids[(wc(h, c, k), p)] = [wc(h, c + 1, 5), wc(h, c, 5)]
-        for k in K4:
-            for h in range(4):
-                for c in (0, 2):
-                    sched[wc(h, c, k)] = mine[k]
-    if VARIANT == "htr":
-        for p in range(P):
-            ki = p % 4
-            k = K4[ki]
-            kids[(ROOT, p)] = [wc(2, 2, k)]
-            for (h, o) in ((2, 3), (1, 0)):
-                relays = [(o, 2), (o, 0), (h, 0), (h, 4)]
-                r = relays[(p // 4 + ki) % 4]
-                kids[(wc(h, 2, k), p)] = ([wc(1, 2, k)] if h == 2 else []) + [wc(r[0], r[1], k), wc(h, 3, 5)] + (
-                    [wc(1, 2, 5)] if h == 1 else [])
-                for e in relays:
-                    kk = []
-                    if e == r:
-                        kk += [wc(q[0], q[1], k) for q in relays[:3] if q != e]
-                    if e != relays[3]:
-                        kk += [wc(e[0], e[1] + 1, 5), wc(e[0], e[1], 5)]
-                    if kk:
-                        kids[(wc(e[0], e[1], k), p)] = kk
-        for k in K4:
-            for h in range(4):
-                for c in (0, 2):
-                    sched[wc(h, c, k)] = mine[k]
-            for h in (2, 1):
-                sched[wc(h, 4, k)] = [[p] for [p] in mine[k] if kids.get((wc(h, 4, k), p))]
+            sched[wc(h, c, 5)] = [list(range(PW * w, PW * w + PW)) for w in range(NW)]
+    for k in HELP:
+        sched[wc(2, 2, k)] = [[] for w in range(NW)]
+    for p in range(P):
+        w, j = divmod(p, PW)
+        helper = wc(2, 2, HELP[j % 4])
+        kids[(ROOT, p)] = [helper]
+        sched[helper][w].append(p)
+        k = K4[(w + j) % 4]
+        far, near = wc(FAR[j][0], FAR[j][1], k), wc(NEAR[j][0], NEAR[j][1], k)
+        kids[(helper, p)] = [far, near]
+        for refl, hosts in ((far, (1, 0)), (near, (2, 3))):
+            ranks = [wc(h, c, 5) for h in hosts for c in range(4) if wc(h, c, 5) != ROOT]
+            s = p % len(ranks)
+            kids[(refl, p)] = ranks[s:] + ranks[:s]
+            sched[refl] = [[p]]
     return kids, sched
 
 
@@ -79,16 +58,6 @@ def transfers(core, grp, kids):
     return [(p, kids[(core, p)], ((1 << e) - 1) << (i * e), e) for i, p in enumerate(send)]
 
 
-def runs(grp):
-    out = []
-    for p in sorted(grp):
-        if out and out[-1][1] == p:
-            out[-1][1] = p + 1
-        else:
-            out.append([p, p + 1])
-    return out
-
-
 def rank_program(g, core, T, topo):
     kids, sched = plan()
     my = sched.get(core)
@@ -100,9 +69,8 @@ def rank_program(g, core, T, topo):
             for (p, dsts, m, e) in transfers(src, grp, kids):
                 if core in dsts:
                     inc[p] = e
-    A = [T.sem.a0, T.sem.a1, T.sem.a2, T.sem.a3, T.sem.a4, T.sem.a5, T.sem.a6, T.sem.a7,
-         T.sem.a8, T.sem.a9, T.sem.a10, T.sem.a11, T.sem.a12, T.sem.a13, T.sem.a14, T.sem.a15]
-    L = [T.sem.l0, T.sem.l1, T.sem.l2, T.sem.l3, T.sem.l4, T.sem.l5, T.sem.l6, T.sem.l7]
+    A = [T.sem.a0, T.sem.a1, T.sem.a2, T.sem.a3]
+    L = [T.sem.l0, T.sem.l1, T.sem.l2, T.sem.l3]
     is_root = core == ROOT
     is_rank = T.rank_of(core) is not None
     sent = stores = 0
@@ -114,8 +82,7 @@ def rank_program(g, core, T, topo):
         if is_root:
             g.wait_ge(L[gi], 16)
         else:
-            for p in grp:
-                g.wait_ge(A[p], inc[p])
+            g.wait_ge(A[grp[0] // PW], sum(inc[p] for p in grp))
         trs = transfers(core, grp, kids)
         if trs:
             calls = []
@@ -124,14 +91,14 @@ def rank_program(g, core, T, topo):
                 for d in dsts:
                     rid, pid = topo.addr(d, core)
                     ids.append(bass.DstId(rid=rid, pnc=pid))
-                calls.append(bass.RemoteDMATransfer(dst_ids=ids, dma_engine_mask=m, remote_sem=A[p],
+                calls.append(bass.RemoteDMATransfer(dst_ids=ids, dma_engine_mask=m, remote_sem=A[p // PW],
                                                     srcs=[T.d[p]], dsts=[T.d[p] for d in dsts]))
                 sent += e
             g.remote_dma_fused(calls, local_sem=T.sem.sent)
         if is_rank and not is_root:
-            for lo, hi in runs(grp):
-                g.dma_start(T.y[lo * R:hi * R, :], T.d[lo:hi]).then_inc(T.sem.st, 16)
-                stores += 1
+            lo, hi = grp[0], grp[-1] + 1
+            g.dma_start(T.y[lo * R:hi * R, :], T.d[lo:hi]).then_inc(T.sem.st, 16)
+            stores += 1
     if is_root:
         g.dma_start(T.y[:, :], T.x[:, :]).then_inc(T.sem.st, 16)
         stores += 1

@@ -25,6 +25,7 @@ def plan():
     for h in range(4):
         for c in range(4):
             sched[wc(h, c, 5)] = [list(range(PW * w, PW * w + PW)) for w in range(NW)]
+    sched[ROOT] = [list(range(0, P // 2)), list(range(P // 2, P))]
     for k in HELP:
         sched[wc(2, 2, k)] = [[] for w in range(NW)]
     for p in range(P):

import concourse.bass as bass
import comms_topo

ROOT = 277
P = 32
NW = 4
PW = P // NW
W = 1024 // P
R = 128 // P
K4 = (2, 3, 6, 7)
HELP = (0, 2, 4, 6)
NEAR = ((3, 0), (3, 2), (3, 4), (3, 6), (2, 0), (2, 4), (2, 6), (2, 8))
FAR = ((1, 2), (1, 0), (1, 4), (1, 6), (1, 8), (1, 10), (1, 12), (1, 14))

SCRATCH = {"d": ("dram", [P, 128, W], "float32")}
SEMAPHORES = ["a0", "a1", "a2", "a3", "l0", "l1", "l2", "l3", "sent", "st"]


def wc(h, c, k):
    return h * 128 + c * 8 + k


def plan():
    kids, sched = {}, {}
    for h in range(4):
        for c in range(4):
            sched[wc(h, c, 5)] = [list(range(PW * w, PW * w + PW)) for w in range(NW)]
    sched[ROOT] = [list(range(0, P // 2)), list(range(P // 2, P))]
    for k in HELP:
        sched[wc(2, 2, k)] = [[] for w in range(NW)]
    for p in range(P):
        w, j = divmod(p, PW)
        helper = wc(2, 2, HELP[j % 4])
        kids[(ROOT, p)] = [helper]
        sched[helper][w].append(p)
        k = K4[(w + j) % 4]
        far, near = wc(FAR[j][0], FAR[j][1], k), wc(NEAR[j][0], NEAR[j][1], k)
        kids[(helper, p)] = [far, near]
        for refl, hosts in ((far, (1, 0)), (near, (2, 3))):
            ranks = [wc(h, c, 5) for h in hosts for c in range(4) if wc(h, c, 5) != ROOT]
            s = p % len(ranks)
            kids[(refl, p)] = ranks[s:] + ranks[:s]
            sched[refl] = [[p]]
    return kids, sched


def transfers(core, grp, kids):
    send = [p for p in grp if kids.get((core, p))]
    if not send:
        return []
    avail = 0xFFFF
    for p in send:
        for d in kids[(core, p)]:
            avail &= comms_topo.mask(core, d)
    n = 16 if avail == 0xFFFF else 8
    e = 1
    while e * 2 * len(send) <= n:
        e *= 2
    return [(p, kids[(core, p)], ((1 << e) - 1) << (i * e), e) for i, p in enumerate(send)]


def rank_program(g, core, T, topo):
    kids, sched = plan()
    my = sched.get(core)
    if not my:
        return
    inc = {}
    for src, groups in sched.items():
        for grp in groups:
            for (p, dsts, m, e) in transfers(src, grp, kids):
                if core in dsts:
                    inc[p] = e
    A = [T.sem.a0, T.sem.a1, T.sem.a2, T.sem.a3]
    L = [T.sem.l0, T.sem.l1, T.sem.l2, T.sem.l3]
    is_root = core == ROOT
    is_rank = T.rank_of(core) is not None
    sent = stores = 0
    if is_root:
        for gi, grp in enumerate(my):
            lo, hi = grp[0], grp[-1] + 1
            g.dma_start(T.d[lo:hi], T.x[lo * R:hi * R, :]).then_inc(L[gi], 16)
    for gi, grp in enumerate(my):
        if is_root:
            g.wait_ge(L[gi], 16)
        else:
            g.wait_ge(A[grp[0] // PW], sum(inc[p] for p in grp))
        trs = transfers(core, grp, kids)
        if trs:
            calls = []
            for (p, dsts, m, e) in trs:
                ids = []
                for d in dsts:
                    rid, pid = topo.addr(d, core)
                    ids.append(bass.DstId(rid=rid, pnc=pid))
                calls.append(bass.RemoteDMATransfer(dst_ids=ids, dma_engine_mask=m, remote_sem=A[p // PW],
                                                    srcs=[T.d[p]], dsts=[T.d[p] for d in dsts]))
                sent += e
            g.remote_dma_fused(calls, local_sem=T.sem.sent)
        if is_rank and not is_root:
            lo, hi = grp[0], grp[-1] + 1
            g.dma_start(T.y[lo * R:hi * R, :], T.d[lo:hi]).then_inc(T.sem.st, 16)
            stores += 1
    if is_root:
        g.dma_start(T.y[:, :], T.x[:, :]).then_inc(T.sem.st, 16)
        stores += 1
    if sent:
        g.wait_ge(T.sem.sent, sent)
    if stores:
        g.wait_ge(T.sem.st, 16 * stores)
